import numpy as np
CORES = [24,48,72,152,176,200]
N = 6
TK = 1024
D = 128 * N
EPS = 0.01
def setup_inputs(rng):
    return {"x": (rng.standard_normal((N, 128, TK), dtype=np.float32) * (0.5 + np.abs(rng.standard_normal((1, 1, TK), dtype=np.float32))) + rng.standard_normal((1, 1, TK), dtype=np.float32))}
def reference(x):
    X = x.astype(np.float64)
    mu = X.sum(axis=(0, 1)) / D
    Z = X - mu
    Z = Z / np.sqrt((Z ** 2).sum(axis=(0, 1)) / D + EPS)
    return {"y": Z.astype(np.float32)}

import math
from concourse.bass import DstId, RemoteDMATransfer
from concourse.mybir import AluOpType, ActivationFunctionType

N = 6
TK = 1024
D = 128 * N
EPS = 0.01
BL = 128
NB = TK // BL
BANK = 512
CH = [4, 4]
LD = [2, 2, 2, 2]
SG = 2
NH = 2

SCRATCH = {
    "xs": ("sbuf", [128, TK], "float32"),
    "idn": ("sbuf", [128, BL + 4], "float32"),
    "pt": ("psum", [128, NB * BANK], "float32"),
    "zt": ("sbuf", [128, TK], "float32"),
    "ys": ("sbuf", [128, TK], "float32"),
    "st": ("sbuf", [128, N * 2 * NB], "float32"),
    "wk": ("sbuf", [128, 7 * 2 * NB], "float32"),
    "hb": ("sbuf", [128, 2 * NB], "float32"),
}
SEMAPHORES = (["cst", "pe", "vc", "sc", "loc", "sto"] + ["ld%d" % i for i in range(len(LD))]
              + ["arr%d" % c for c in range(len(CH))] + ["hin%d" % c for c in range(len(CH))])


def _bits(mask):
    return [e for e in range(32) if (mask >> e) & 1]


def _mask(engines):
    m = 0
    for e in engines:
        m |= 1 << e
    return m


def _plan(T, topo, r):
    c = T.cores[r]
    ncores = (max(topo.host(k) for k in T.cores) + 1) * topo.CORES_PER_HOST
    direct = [q for q in range(N) if q != r and topo.may_write(c, T.cores[q])]
    cross = [q for q in range(N) if q != r and q not in direct]
    cand = [k for k in range(ncores)
            if k not in T.cores and topo.host(k) == topo.host(c) and topo.chip(k) == topo.chip(c)
            and topo.die(k) == topo.die(c) and all(topo.may_write(k, T.cores[q]) for q in cross)]
    nh = min(NH, len(cand), len(cross))
    helpers = [(cand[i], cross[i::nh]) for i in range(nh)]
    return direct, helpers


def _groups():
    out, j0, off = [], 0, 0
    for nb in CH:
        out.append((j0, nb, off))
        j0 += nb
        off += N * 2 * nb
    return out


def _send(g, T, topo, core, src, dsts, dst_ap, engines, remote_sem):
    ids = []
    for d in dsts:
        rid, pid = topo.addr(d, core)
        ids.append(DstId(rid=rid, pnc=pid))
    g.remote_dma_fused([RemoteDMATransfer(dst_ids=ids, dma_engine_mask=_mask(engines), remote_sem=remote_sem,
                                          srcs=[src], dsts=[dst_ap for _ in dsts])], local_sem=T.sem.loc)
    return len(engines)


def _on_only(T, topo, r):
    c = T.cores[r]
    direct, helpers = _plan(T, topo, r)
    on = topo.mask(c, helpers[0][0])
    off = topo.mask(c, T.cores[direct[0]])
    return _bits(on & ~off)


def _helper_program(g, core, T, topo, r, serves):
    sent = 0
    hoff = 0
    n_on = len(_on_only(T, topo, r))
    for c, (j0, nb, off) in enumerate(_groups()):
        w = 2 * nb
        g.wait_ge(T.sem["hin%d" % c], n_on)
        eng = _bits(topo.mask(core, T.cores[serves[0]]))
        sent += _send(g, T, topo, core, T.hb[:, hoff:hoff + w], [T.cores[q] for q in serves],
                      T.st[:, off + r * w:off + (r + 1) * w], eng, T.sem["arr%d" % c])
        hoff += w
    g.wait_ge(T.sem.loc, sent)


def rank_program(g, core, T, topo):
    rank = T.rank_of(core)
    if rank is None:
        for r in range(N):
            for h, serves in _plan(T, topo, r)[1]:
                if h == core:
                    _helper_program(g, core, T, topo, r, serves)
        return

    V, S, PE, SY = g.vector, g.scalar, g.tensor, g.sync
    sem = T.sem
    A = AluOpType
    F = ActivationFunctionType
    cnt = {"pe": 0, "vc": 0, "sc": 0}
    groups = _groups()
    direct, helpers = _plan(T, topo, rank)

    arrive = 0
    for q in range(N):
        if q == rank:
            continue
        dq, hq = _plan(T, topo, q)
        if rank in dq:
            arrive += len(_bits(topo.mask(T.cores[q], core)))
        else:
            for h, serves in hq:
                if rank in serves:
                    arrive += len(_bits(topo.mask(h, core)))

    j = 0
    load_of = {}
    for i, nb in enumerate(LD):
        SY.dma_start(T.xs[:, j * BL:(j + nb) * BL], T.x[:, j * BL:(j + nb) * BL]).then_inc(sem["ld%d" % i], 16)
        for k in range(j, j + nb):
            load_of[k] = i
        j += nb

    V.memset(T.idn[:, 0:BL], 1.0).then_inc(sem.cst, 1)
    V.memset(T.idn[:, BL:BL + 1], 1.0 / D).then_inc(sem.cst, 1)
    g.wait_ge(sem.cst, 2)
    g.affine_select(T.idn[:, 0:BL], T.idn[:, 0:BL], [[-1, BL]], A.is_equal, 0.0, 0, 1).then_inc(sem.cst, 1)
    PE.wait_ge(sem.cst, 3)

    sent = 0
    hoff = 0
    ready = []
    seen = -1
    for c, (j0, nb, off) in enumerate(groups):
        w = 2 * nb
        o = off + rank * w
        for jj in range(nb):
            j = j0 + jj
            if load_of[j] != seen:
                seen = load_of[j]
                PE.wait_ge(sem["ld%d" % seen], 16)
            PE.matmul(T.pt[:, j * BANK:j * BANK + BL + 1], T.xs[:, j * BL:(j + 1) * BL], T.idn[:, 0:BL + 1],
                      True, True).then_inc(sem.pe, 1)
            cnt["pe"] += 1
            V.wait_ge(sem.pe, cnt["pe"])
            V.tensor_copy(T.st[:, o + jj:o + jj + 1], T.pt[:, j * BANK + BL:j * BANK + BL + 1]).then_inc(sem.vc, 1)
            cnt["vc"] += 1
            S.wait_ge(sem.vc, cnt["vc"])
            S.activation(T.zt[:, j * BL:(j + 1) * BL], T.pt[:, j * BANK:j * BANK + BL], F.Square,
                         scale=1.0 / math.sqrt(D), accum_out=T.st[:, o + nb + jj:o + nb + jj + 1]).then_inc(sem.sc, 1)
            cnt["sc"] += 1
        ready.append((cnt["vc"], cnt["sc"]))
        g.wait_ge(sem.vc, cnt["vc"])
        g.wait_ge(sem.sc, cnt["sc"])
        piece = T.st[:, o:o + w]
        sent += _send(g, T, topo, core, piece, [h for h, _ in helpers], T.hb[:, hoff:hoff + w],
                      _on_only(T, topo, rank), sem["hin%d" % c])
        sent += _send(g, T, topo, core, piece, [T.cores[q] for q in direct], piece,
                      _bits(topo.mask(core, T.cores[direct[0]])), sem["arr%d" % c])
        hoff += w

    def vop(ins):
        ins.then_inc(sem.vc, 1)
        cnt["vc"] += 1

    copies = []

    def flush():
        for (j, pe_at) in copies:
            S.wait_ge(sem.pe, pe_at)
            S.activation(T.ys[:, j * BL:(j + 1) * BL], T.pt[:, j * BANK:j * BANK + BL], F.Copy).then_inc(sem.sc, 1)
            cnt["sc"] += 1
            if (j + 1) % SG == 0:
                SY.wait_ge(sem.sc, cnt["sc"])
                SY.dma_start(T.y[:, (j + 1 - SG) * BL:(j + 1) * BL],
                             T.ys[:, (j + 1 - SG) * BL:(j + 1) * BL]).then_inc(sem.sto, 16)
        del copies[:]

    wo = 0
    for c, (j0, nb, off) in enumerate(groups):
        w = 2 * nb
        a = T.wk[:, wo:wo + 3 * w]
        b = T.wk[:, wo + 3 * w:wo + 4 * w]
        tot = wo + 4 * w
        msq = T.wk[:, wo + 5 * w:wo + 5 * w + nb]
        var = T.wk[:, wo + 5 * w + nb:wo + 6 * w]
        sd = T.wk[:, wo + 6 * w:wo + 6 * w + nb]
        rs = wo + 6 * w + nb
        wo += 7 * w
        V.wait_ge(sem["arr%d" % c], arrive)
        V.wait_ge(sem.vc, ready[c][0])
        V.wait_ge(sem.sc, ready[c][1])
        vop(V.tensor_tensor(a, T.st[:, off:off + 3 * w], T.st[:, off + 3 * w:off + 6 * w], A.add))
        V.wait_ge(sem.vc, cnt["vc"])
        vop(V.tensor_tensor(b, T.wk[:, tot - 4 * w:tot - 3 * w], T.wk[:, tot - 3 * w:tot - 2 * w], A.add))
        V.wait_ge(sem.vc, cnt["vc"])
        vop(V.tensor_tensor(T.wk[:, tot:tot + w], b, T.wk[:, tot - 2 * w:tot - w], A.add))
        V.wait_ge(sem.vc, cnt["vc"])
        vop(V.tensor_tensor(msq, T.wk[:, tot:tot + nb], T.wk[:, tot:tot + nb], A.mult))
        V.wait_ge(sem.vc, cnt["vc"])
        vop(V.tensor_tensor(var, T.wk[:, tot + nb:tot + w], msq, A.subtract))
        S.wait_ge(sem.vc, cnt["vc"])
        S.activation(sd, var, F.Sqrt, bias=EPS).then_inc(sem.sc, 1)
        cnt["sc"] += 1
        V.wait_ge(sem.sc, cnt["sc"])
        flush()
        vop(V.reciprocal(T.wk[:, rs:rs + nb], sd))
        V.wait_ge(sem.vc, cnt["vc"])
        for jj in range(nb):
            j = j0 + jj
            vop(V.tensor_scalar(T.zt[:, j * BL:(j + 1) * BL], T.pt[:, j * BANK:j * BANK + BL],
                                T.wk[:, tot + jj:tot + jj + 1], T.wk[:, rs + jj:rs + jj + 1], A.subtract, A.mult))
            PE.wait_ge(sem.vc, cnt["vc"])
            PE.matmul(T.pt[:, j * BANK:j * BANK + BL], T.zt[:, j * BL:(j + 1) * BL], T.idn[:, 0:BL],
                      True, True).then_inc(sem.pe, 1)
            cnt["pe"] += 1
            copies.append((j, cnt["pe"]))
    flush()
    SY.wait_ge(sem.sto, 16 * (NB // SG))
    g.wait_ge(sem.loc, sent)
